import numpy as np
import ml_dtypes


def mxq(x, axis, fmt="e4m3"):
    dtype, down = {"e4m3": (ml_dtypes.float8_e4m3fn, 7), "e5m2": (ml_dtypes.float8_e5m2, 14)}[fmt]
    v = np.moveaxis(np.asarray(x, np.float32).astype(ml_dtypes.bfloat16).astype(np.float64), axis, -1)
    blocks = v.reshape(v.shape[:-1] + (-1, 32))
    amax = np.abs(blocks).max(-1, keepdims=True)
    byte = np.maximum(np.where(amax > 0, np.frexp(amax)[1] - 1 + 127, 0) - down, 1)
    scale = np.exp2(byte - 127.0)
    codes = (blocks / scale).astype(np.float32).astype(dtype).astype(np.float64)
    return np.moveaxis((codes * scale).reshape(v.shape), -1, axis)


WIDE = False


def mx_kscale(k):
    if not WIDE:
        return np.ones(k)
    levels = np.array([30, -30])
    if k % 512:
        return np.exp2(np.random.permutation(np.resize(levels, k // 32))).repeat(32)
    a = np.empty((k // 512, 16))
    for p in range(k // 512):
        a[p, :8] = np.random.permutation(np.resize(levels, 8))
        for g in range(8):
            far = levels[np.abs(levels - a[p, g]) >= 10]
            a[p, g + 8] = far[np.random.randint(len(far))]
    return np.exp2(a.ravel()).repeat(32)


def f64(x):
    return np.asarray(x).astype(np.float64)


def striped(idx):
    return np.tile(np.asarray(idx).reshape(-1, 16).T, (8, 1)).astype(np.uint16)


def unstriped(offs):
    return offs[:16].T.reshape(-1).astype(np.int64)


def bf(x):
    return np.asarray(x, np.float32).astype(ml_dtypes.bfloat16)


def planes(Y):
    r, m = Y.shape
    b = f64(bf(Y)).reshape(r // 32, 32, m)
    amax = np.abs(b).max(1)
    byte = np.clip(np.where(amax > 0, np.frexp(amax)[1] - 1 + 127 - 7, 1), 1, 254)
    codes = (b * np.exp2(127.0 - byte)[:, None, :]).reshape(r, m).astype(np.float32).astype(ml_dtypes.float8_e4m3fn).view(np.uint8)
    words = codes.reshape(r // 512, 128, 4, m).transpose(0, 1, 3, 2)
    return np.ascontiguousarray(words), np.ascontiguousarray(byte.astype(np.uint8).reshape(r // 512, 16, m))


K, J, N, T, V = 512, 512, 256, 1024, 1024


def setup_inputs():
    n = np.random.standard_normal
    idx = np.random.permutation(T)[:J]
    idx2 = np.random.permutation(V)[:J]
    fj = mx_kscale(J)
    return {
        "xf": (n((K, T))).astype(np.float32),
        "ra": (np.random.uniform(0.5, 1.5, (1, J)) * fj).astype(np.float32),
        "gt": (n((N, V)) * np.exp(0.5 * n((1, V)))).astype(np.float32),
        "cb": (np.random.uniform(0.5, 1.5, (J, 1)) / fj[:, None]).astype(np.float32),
        "bn": (np.random.uniform(-0.5, 0.5, (1, N))).astype(np.float32),
        "offs": striped(idx),
        "offs2": striped(idx2),
    }


def reference(xf, ra, gt, cb, bn, offs, offs2):
    idx = unstriped(offs)
    idx2 = unstriped(offs2)
    xg = f64(xf)[:, idx]
    x1 = np.pad(xg, ((0, 0), (1, 0)))[:, :J]
    us = (xg - 0.6 * x1) * f64(ra)
    uj = us.T
    gr1 = f64(gt)[:, idx2].T
    gj = gr1 / (np.max(np.abs(gr1), axis=1, keepdims=True) + 0.2) * f64(cb)
    ujq = mxq(uj, 0, "e5m2")
    gjq = mxq(gj, 0, "e5m2")
    w = ujq.T @ gjq
    ew = np.exp(0.02 * w + f64(bn))
    y = 256.0 * ew / np.sum(ew, axis=1, keepdims=True)
    words, scales = planes(y)
    return y, words, scales

@@ -1,0 +1,250 @@
+from contextlib import ExitStack
+
+import concourse.mybir as mybir
+from concourse.masks import make_identity
+
+K, J, N, T, V = 512, 512, 256, 1024, 1024
+FLOPS = 2 * K * J * N
+
+F32 = mybir.dt.float32
+BF16 = mybir.dt.bfloat16
+U32 = mybir.dt.uint32
+I32 = mybir.dt.int32
+U16 = mybir.dt.uint16
+U8 = mybir.dt.uint8
+E5M2X4 = mybir.dt.float8_e5m2_x4
+E4M3X4 = mybir.dt.float8_e4m3fn_x4
+ALU = mybir.AluOpType
+ACT = mybir.ActivationFunctionType
+AXIS_X = mybir.AxisListType.X
+
+P = 128
+PACK = 4
+PAD = 8
+LIST_COLS = J // 16
+SPLIT_G = (0, 1)
+SPLIT_X = (0,)
+SUM_ON_TENSOR = ()
+WEIGH_ON_SCALAR = (1, 2)
+RING = 2
+SHARES_ON_SCALAR = ()
+ROUND_SPLIT = 176
+
+
+def tile_list_moment_steps_sized_shares_pl_kernel(tc, xf, ra, gt, cb, bn, offs, offs2, out_0, out_1, out_2):
+    nc = tc.nc
+    with ExitStack() as ctx:
+        keep = ctx.enter_context(tc.tile_pool(name="keep", bufs=1))
+        turn = ctx.enter_context(tc.psum_pool(name="turn", bufs=5))
+        acc = ctx.enter_context(tc.psum_pool(name="acc", bufs=3))
+
+        g_list = keep.tile([P, LIST_COLS], U16, name="g_list")
+        x_list = keep.tile([P, LIST_COLS], U16, name="x_list")
+        g_tab = [keep.tile([P, V], F32, name=f"g_tab{h}") for h in range(2)]
+        x_tab = [keep.tile([P, T], F32, name=f"x_tab{i}") for i in range(PACK)]
+        bn_pairs = keep.tile([P, 2], F32, name="bn_pairs")
+        cb_sb = keep.tile([P, PACK], F32, name="cb_sb")
+        ra_sb = keep.tile([P, PACK], F32, name="ra_sb")
+
+        x_rows = xf.rearrange("(p i) c -> p i c", i=PACK)
+        nc.sync.dma_start(g_list[:], offs2)
+        for h in range(2):
+            nc.sync.dma_start(g_tab[h][:], gt[h * P : (h + 1) * P, :])
+        nc.sync.dma_start(x_list[:], offs)
+        nc.scalar.dma_start(bn_pairs[:], bn.rearrange("o (p e) -> (o p) e", e=2))
+        nc.scalar.dma_start(cb_sb[:], cb.rearrange("(p t) o -> p (t o)", t=PACK))
+        nc.scalar.dma_start(ra_sb[:], ra.rearrange("o (p t) -> (o p) t", t=PACK))
+        for i in range(PACK):
+            nc.sync.dma_start(x_tab[i][:], x_rows[:, i, :])
+
+        ident = keep.tile([P, P], F32, name="ident")
+        make_identity(nc, ident[:])
+
+        bn_ps = turn.tile([P, 2, P], F32, name="bn_ps", tag="turn")
+        for e in range(2):
+            nc.tensor.transpose(bn_ps[:, e, :], bn_pairs[:, e : e + 1].to_broadcast([P, P]), ident[:])
+        bn_row = keep.tile([P, N], F32, name="bn_row")
+        nc.vector.tensor_copy(
+            out=bn_row[:].rearrange("p (m e) -> p m e", e=2), in_=bn_ps[:].rearrange("p e m -> p m e")
+        )
+
+        def gather(dst, table, lst, split):
+            half = LIST_COLS // 2
+            if split:
+                nc.scalar.activation(dst[:, 0 : J // 2], table[:].indirect(lst[:, 0:half]), ACT.Copy)
+                nc.vector.tensor_copy(dst[:, J // 2 : J], table[:].indirect(lst[:, half:LIST_COLS]))
+            else:
+                nc.scalar.activation(dst, table[:].indirect(lst[:]), ACT.Copy)
+
+        g_ps = []
+        g_abs0 = keep.tile([P, PACK, P], F32, name="g_abs0")
+        g_abs1 = keep.tile([P, PACK, P + PACK], F32, name="g_abs1")
+        g_max = keep.tile([P, PACK], F32, name="g_max")
+        g_codes = keep.tile([P, N], U32, name="g_codes", align_bytes=64)
+        g_scales = keep.tile([P, N], U8, name="g_scales", align_bytes=64)
+        y = keep.tile([P, PACK, N], F32, name="y")
+        y_rows = out_0.rearrange("(p i) n -> p i n", i=PACK)
+        g_picked, x_picked, x_ps, u_codes, u_scales, ew, total = {}, {}, {}, {}, {}, {}, {}
+
+        ring = [keep.tile([P, PAD + J], F32, name=f"picked{b}") for b in range(RING)]
+        zero = keep.tile([P, 1], F32, name="zero")
+        nc.vector.memset(zero[:], 0.0)
+        for b in range(RING):
+            nc.scalar.activation(ring[b][:, PAD - 1 : PAD], zero[:], ACT.Copy)
+
+        def pick_g(h):
+            g_picked[h] = ring[h % RING]
+            gather(g_picked[h][:, PAD : PAD + J], g_tab[h], g_list, h in SPLIT_G)
+
+        def turn_g(h):
+            bank = turn.tile([P, PACK, P], F32, name=f"g_ps{h}", tag="turn")
+            for t in range(PACK):
+                nc.tensor.transpose(bank[:, t, :], g_picked[h][:, PAD + t : PAD + J : PACK], ident[:])
+            g_ps.append(bank)
+            if h == 0:
+                nc.scalar.activation(g_abs0[:], bank[:], ACT.Abs)
+                nc.vector.tensor_reduce(g_abs1[:, :, P], g_abs0[:], AXIS_X, ALU.max)
+            else:
+                nc.scalar.activation(g_abs1[:, :, 0:P], bank[:], ACT.Abs)
+                nc.vector.tensor_reduce(g_max[:], g_abs1[:, :, 0 : P + 1], AXIS_X, ALU.max)
+
+        def quantise_g():
+            g_den = keep.tile([P, PACK], F32, name="g_den")
+            g_inv = keep.tile([P, PACK], F32, name="g_inv")
+            g_fac = keep.tile([P, PACK], F32, name="g_fac")
+            nc.vector.tensor_scalar(g_den[:], g_max[:], 0.2, None, ALU.add)
+            nc.vector.reciprocal(g_inv[:], g_den[:])
+            nc.vector.tensor_tensor(g_fac[:], g_inv[:], cb_sb[:], ALU.mult)
+            g_bf = keep.tile([P, N, PACK], BF16, name="g_bf", align_bytes=64)
+            for h in range(2):
+                nc.vector.tensor_tensor(
+                    g_bf[:, h * P : (h + 1) * P, :],
+                    g_ps[h][:].rearrange("p t n -> p n t"),
+                    g_fac[:].unsqueeze(1).to_broadcast([P, P, PACK]),
+                    ALU.mult,
+                )
+            nc.vector.quantize_mx(g_codes[:].bitcast(E5M2X4), g_scales[:], g_bf[:].rearrange("p n t -> p (n t)"))
+
+        def pick_x(i):
+            x_picked[i] = ring[(2 + i) % RING]
+            gather(x_picked[i][:, PAD : PAD + J], x_tab[i], x_list, i in SPLIT_X)
+
+        def step_x(i):
+            picked = x_picked[i]
+            step = keep.tile([P, PACK, P], F32, name=f"step{i}")
+            before = picked[:, PAD - 1 : PAD - 1 + J].rearrange("p (q t) -> p q t", t=PACK)
+            x_ps[i] = turn.tile([P, PACK, P], F32, name=f"x_ps{i}", tag="turn")
+            if i in SUM_ON_TENSOR:
+                nc.scalar.activation(step[:].rearrange("p t q -> p q t"), before, ACT.Copy, scale=-0.6)
+                for t in range(PACK):
+                    nc.tensor.matmul(
+                        x_ps[i][:, t, :], picked[:, PAD + t : PAD + J : PACK], ident[:],
+                        start=(t == 0), stop=False, is_transpose=True,
+                    )
+                for t in range(PACK):
+                    nc.tensor.matmul(
+                        x_ps[i][:, t, :], step[:, t, :], ident[:],
+                        start=False, stop=(t == PACK - 1), is_transpose=True,
+                    )
+            else:
+                nc.vector.scalar_tensor_tensor(
+                    step[:].rearrange("p t q -> p q t"),
+                    before,
+                    -0.6,
+                    picked[:, PAD : PAD + J].rearrange("p (q t) -> p q t", t=PACK),
+                    ALU.mult,
+                    ALU.add,
+                )
+                for t in range(PACK):
+                    nc.tensor.transpose(x_ps[i][:, t, :], step[:, t, :], ident[:])
+
+        def quantise_x(i):
+            u_bf = keep.tile([P, P, PACK], BF16, name=f"u_bf{i}", align_bytes=64)
+            if i in WEIGH_ON_SCALAR:
+                planes = keep.tile([P, PACK, P], BF16, name=f"u_planes{i}")
+                for t in range(PACK):
+                    nc.scalar.activation(planes[:, t, :], x_ps[i][:, t, :], ACT.Copy, scale=ra_sb[:, t : t + 1])
+                nc.scalar.copy(u_bf[:], planes[:].rearrange("p t m -> p m t"))
+            else:
+                nc.vector.tensor_tensor(
+                    u_bf[:],
+                    x_ps[i][:].rearrange("p t m -> p m t"),
+                    ra_sb[:].unsqueeze(1).to_broadcast([P, P, PACK]),
+                    ALU.mult,
+                )
+            u_codes[i] = keep.tile([P, P], U32, name=f"u_codes{i}", align_bytes=64)
+            u_scales[i] = keep.tile([P, P], U8, name=f"u_scales{i}", align_bytes=64)
+            nc.vector.quantize_mx(
+                u_codes[i][:].bitcast(E5M2X4), u_scales[i][:], u_bf[:].rearrange("p m t -> p (m t)")
+            )
+
+        def product(i):
+            w = acc.tile([P, N], F32, name=f"w{i}", tag="w")
+            nc.tensor.matmul_mx(
+                out=w[:],
+                lhsT=u_codes[i][:].bitcast(E5M2X4),
+                lhsT_scale=u_scales[i][:],
+                rhs=g_codes[:].bitcast(E5M2X4),
+                rhs_scale=g_scales[:],
+                start=True,
+                stop=True,
+            )
+            neg_z = keep.tile([P, N], F32, name=f"neg_z{i}")
+            nc.vector.scalar_tensor_tensor(neg_z[:], w[:], -0.02, bn_row[:], ALU.mult, ALU.subtract)
+            neg_top = keep.tile([P, 1], F32, name=f"neg_top{i}")
+            nc.vector.tensor_reduce(neg_top[:], neg_z[:], AXIS_X, ALU.min)
+            ew[i] = keep.tile([P, N], F32, name=f"ew{i}")
+            total[i] = keep.tile([P, 1], F32, name=f"total{i}")
+            nc.scalar.activation(ew[i][:], neg_z[:], ACT.Exp, bias=neg_top[:], scale=-1.0, accum_out=total[i][:])
+
+        def shares(i):
+            inv = keep.tile([P, 1], F32, name=f"inv{i}")
+            if i in SHARES_ON_SCALAR:
+                part = keep.tile([P, 1], F32, name=f"part{i}")
+                nc.scalar.activation(part[:], total[i][:], ACT.Copy, scale=1.0 / 256.0)
+                nc.vector.reciprocal(inv[:], part[:])
+                nc.scalar.activation(y[:, i, :], ew[i][:], ACT.Copy, scale=inv[:])
+            else:
+                nc.vector.reciprocal(inv[:], total[i][:])
+                nc.vector.tensor_scalar(y[:, i, :], ew[i][:], inv[:], 256.0, ALU.mult, ALU.mult)
+            nc.sync.dma_start(y_rows[:, i, :], y[:, i, :])
+
+        pick_g(0)
+        turn_g(0)
+        pick_g(1)
+        turn_g(1)
+        quantise_g()
+        pick_x(0)
+        step_x(0)
+        quantise_x(0)
+        pick_x(1)
+        step_x(1)
+        quantise_x(1)
+        pick_x(2)
+        step_x(2)
+        quantise_x(2)
+        pick_x(3)
+        step_x(3)
+        quantise_x(3)
+        product(0)
+        product(1)
+        product(2)
+        product(3)
+        shares(0)
+        shares(1)
+        shares(2)
+        shares(3)
+
+        y_bf = keep.tile([P, N, PACK], BF16, name="y_bf", align_bytes=64)
+        y_codes = keep.tile([P, N], U32, name="y_codes", align_bytes=64)
+        y_scales = keep.tile([P, N], U8, name="y_scales", align_bytes=64)
+        y_turned = y[:].rearrange("p i n -> p n i")
+        nc.vector.tensor_copy(y_bf[:, 0:ROUND_SPLIT, :], y_turned[:, 0:ROUND_SPLIT, :])
+        nc.scalar.copy(y_bf[:, ROUND_SPLIT:N, :], y_turned[:, ROUND_SPLIT:N, :])
+        nc.vector.quantize_mx(y_codes[:].bitcast(E4M3X4), y_scales[:], y_bf[:].rearrange("p n i -> p (n i)"))
+        nc.sync.dma_start(out_1[0].rearrange("p c r -> p (c r)").bitcast(I32), y_codes[:].bitcast(I32))
+        for q in range(4):
+            queue = nc.scalar if q % 2 == 0 else nc.sync
+            queue.dma_start(
+                out_2[0, 4 * q : 4 * q + 4, :].bitcast(I32), y_scales[32 * q : 32 * q + 4, :].bitcast(I32)
+            )

@@ -28,6 +28,9 @@ SUM_ON_TENSOR = ()
 WEIGH_ON_SCALAR = (1, 2)
 RING = 2
 SHARES_ON_SCALAR = ()
+HALVED = ()
+ON_VECTOR = ()
+STEPPED_TURN = (0, 1, 2)
 ROUND_SPLIT = 176
 
 
@@ -127,7 +130,17 @@ def tile_list_moment_steps_sized_shares_pl_kernel(tc, xf, ra, gt, cb, bn, offs, 
 
         def pick_x(i):
             x_picked[i] = ring[(2 + i) % RING]
-            gather(x_picked[i][:, PAD : PAD + J], x_tab[i], x_list, i in SPLIT_X)
+            if i in HALVED:
+                for a in range(2):
+                    nc.scalar.activation(
+                        x_picked[i][:, PAD + a * J // 2 : PAD + (a + 1) * J // 2],
+                        x_tab[i][:].indirect(x_list[:, a * LIST_COLS // 2 : (a + 1) * LIST_COLS // 2]),
+                        ACT.Copy,
+                    )
+            elif i in ON_VECTOR:
+                nc.vector.tensor_copy(x_picked[i][:, PAD : PAD + J], x_tab[i][:].indirect(x_list[:]))
+            else:
+                gather(x_picked[i][:, PAD : PAD + J], x_tab[i], x_list, i in SPLIT_X)
 
         def step_x(i):
             picked = x_picked[i]
@@ -146,15 +159,25 @@ def tile_list_moment_steps_sized_shares_pl_kernel(tc, xf, ra, gt, cb, bn, offs, 
                         x_ps[i][:, t, :], step[:, t, :], ident[:],
                         start=False, stop=(t == PACK - 1), is_transpose=True,
                     )
-            else:
+            elif i in STEPPED_TURN:
+                flat = step[:].rearrange("p t q -> p (t q)")
                 nc.vector.scalar_tensor_tensor(
-                    step[:].rearrange("p t q -> p q t"),
-                    before,
-                    -0.6,
-                    picked[:, PAD : PAD + J].rearrange("p (q t) -> p q t", t=PACK),
-                    ALU.mult,
-                    ALU.add,
+                    flat, picked[:, PAD - 1 : PAD - 1 + J], -0.6, picked[:, PAD : PAD + J], ALU.mult, ALU.add
                 )
+                for t in range(PACK):
+                    nc.tensor.transpose(x_ps[i][:, t, :], flat[:, t::PACK], ident[:])
+            else:
+                parts = 2 if i in HALVED else 1
+                for a in range(parts):
+                    qs = slice(a * P // parts, (a + 1) * P // parts)
+                    nc.vector.scalar_tensor_tensor(
+                        step[:].rearrange("p t q -> p q t")[:, qs, :],
+                        before[:, qs, :],
+                        -0.6,
+                        picked[:, PAD : PAD + J].rearrange("p (q t) -> p q t", t=PACK)[:, qs, :],
+                        ALU.mult,
+                        ALU.add,
+                    )
                 for t in range(PACK):
                     nc.tensor.transpose(x_ps[i][:, t, :], step[:, t, :], ident[:])
 

@@ -24,13 +24,13 @@ PAD = 8
 LIST_COLS = J // 16
 SPLIT_G = (0, 1)
 SPLIT_X = (0,)
-SUM_ON_TENSOR = ()
-WEIGH_ON_SCALAR = (1, 2)
+SUM_ON_TENSOR = (3,)
+WEIGH_ON_SCALAR = (1,)
 RING = 2
-SHARES_ON_SCALAR = ()
+SHARES_ON_SCALAR = (0,)
 HALVED = ()
 ON_VECTOR = ()
-STEPPED_TURN = (0, 1, 2)
+STEPPED_TURN = ()
 ROUND_SPLIT = 176
 
 
@@ -81,7 +81,7 @@ def tile_list_moment_steps_sized_shares_pl_kernel(tc, xf, ra, gt, cb, bn, offs, 
 
         g_ps = []
         g_abs0 = keep.tile([P, PACK, P], F32, name="g_abs0")
-        g_abs1 = keep.tile([P, PACK, P + PACK], F32, name="g_abs1")
+        g_abs1 = keep.tile([P, PACK, P + PACK], F32, name="g_abs1", tag="shared")
         g_max = keep.tile([P, PACK], F32, name="g_max")
         g_codes = keep.tile([P, N], U32, name="g_codes", align_bytes=64)
         g_scales = keep.tile([P, N], U8, name="g_scales", align_bytes=64)
@@ -111,13 +111,16 @@ def tile_list_moment_steps_sized_shares_pl_kernel(tc, xf, ra, gt, cb, bn, offs, 
                 nc.scalar.activation(g_abs1[:, :, 0:P], bank[:], ACT.Abs)
                 nc.vector.tensor_reduce(g_max[:], g_abs1[:, :, 0 : P + 1], AXIS_X, ALU.max)
 
-        def quantise_g():
+        g_fac = keep.tile([P, PACK], F32, name="g_fac")
+
+        def factor_g():
             g_den = keep.tile([P, PACK], F32, name="g_den")
             g_inv = keep.tile([P, PACK], F32, name="g_inv")
-            g_fac = keep.tile([P, PACK], F32, name="g_fac")
-            nc.vector.tensor_scalar(g_den[:], g_max[:], 0.2, None, ALU.add)
-            nc.vector.reciprocal(g_inv[:], g_den[:])
-            nc.vector.tensor_tensor(g_fac[:], g_inv[:], cb_sb[:], ALU.mult)
+            nc.vector.reciprocal(g_inv[:], cb_sb[:])
+            nc.vector.scalar_tensor_tensor(g_den[:], g_max[:], 0.2, g_inv[:], ALU.add, ALU.mult)
+            nc.vector.reciprocal(g_fac[:], g_den[:])
+
+        def quantise_g():
             g_bf = keep.tile([P, N, PACK], BF16, name="g_bf", align_bytes=64)
             for h in range(2):
                 nc.vector.tensor_tensor(
@@ -144,7 +147,7 @@ def tile_list_moment_steps_sized_shares_pl_kernel(tc, xf, ra, gt, cb, bn, offs, 
 
         def step_x(i):
             picked = x_picked[i]
-            step = keep.tile([P, PACK, P], F32, name=f"step{i}")
+            step = keep.tile([P, PACK, P], F32, name=f"step{i}", tag="shared" if i == 1 else f"step{i}")
             before = picked[:, PAD - 1 : PAD - 1 + J].rearrange("p (q t) -> p q t", t=PACK)
             x_ps[i] = turn.tile([P, PACK, P], F32, name=f"x_ps{i}", tag="turn")
             if i in SUM_ON_TENSOR:
@@ -236,26 +239,27 @@ def tile_list_moment_steps_sized_shares_pl_kernel(tc, xf, ra, gt, cb, bn, offs, 
         turn_g(0)
         pick_g(1)
         turn_g(1)
-        quantise_g()
+        factor_g()
         pick_x(0)
         step_x(0)
         quantise_x(0)
         pick_x(1)
         step_x(1)
-        quantise_x(1)
         pick_x(2)
         step_x(2)
-        quantise_x(2)
         pick_x(3)
         step_x(3)
+        quantise_g()
+        quantise_x(2)
         quantise_x(3)
+        quantise_x(1)
         product(0)
-        product(1)
         product(2)
+        product(1)
         product(3)
         shares(0)
-        shares(1)
         shares(2)
+        shares(1)
         shares(3)
 
         y_bf = keep.tile([P, N, PACK], BF16, name="y_bf", align_bytes=64)

@@ -55,9 +55,10 @@ def tile_list_moment_steps_sized_shares_pl_kernel(tc, xf, ra, gt, cb, bn, offs, 
             nc.sync.dma_start(g_tab[h][:], gt[h * P : (h + 1) * P, :])
         nc.sync.dma_start(x_list[:], offs)
         nc.scalar.dma_start(bn_pairs[:], bn.rearrange("o (p e) -> (o p) e", e=2))
-        nc.scalar.dma_start(cb_sb[:], cb.rearrange("(p t) o -> p (t o)", t=PACK))
-        nc.scalar.dma_start(ra_sb[:], ra.rearrange("o (p t) -> (o p) t", t=PACK))
-        for i in range(PACK):
+        nc.sync.dma_start(x_tab[0][:], x_rows[:, 0, :])
+        nc.sync.dma_start(cb_sb[:], cb.rearrange("(p t) o -> p (t o)", t=PACK))
+        nc.sync.dma_start(ra_sb[:], ra.rearrange("o (p t) -> (o p) t", t=PACK))
+        for i in range(1, PACK):
             nc.sync.dma_start(x_tab[i][:], x_rows[:, i, :])
 
         ident = keep.tile([P, P], F32, name="ident")
@@ -190,7 +191,9 @@ def tile_list_moment_steps_sized_shares_pl_kernel(tc, xf, ra, gt, cb, bn, offs, 
                 planes = keep.tile([P, PACK, P], BF16, name=f"u_planes{i}")
                 for t in range(PACK):
                     nc.scalar.activation(planes[:, t, :], x_ps[i][:, t, :], ACT.Copy, scale=ra_sb[:, t : t + 1])
-                nc.scalar.copy(u_bf[:], planes[:].rearrange("p t m -> p m t"))
+                nc.scalar.copy(
+                    u_bf[:].rearrange("p (c e) t -> p c t e", e=PACK), planes[:].rearrange("p t (c e) -> p c t e", e=PACK)
+                )
             else:
                 nc.vector.tensor_tensor(
                     u_bf[:],
@@ -233,7 +236,6 @@ def tile_list_moment_steps_sized_shares_pl_kernel(tc, xf, ra, gt, cb, bn, offs, 
             else:
                 nc.vector.reciprocal(inv[:], total[i][:])
                 nc.vector.tensor_scalar(y[:, i, :], ew[i][:], inv[:], 256.0, ALU.mult, ALU.mult)
-            nc.sync.dma_start(y_rows[:, i, :], y[:, i, :])
 
         pick_g(0)
         turn_g(0)
@@ -259,15 +261,19 @@ def tile_list_moment_steps_sized_shares_pl_kernel(tc, xf, ra, gt, cb, bn, offs, 
         product(3)
         shares(0)
         shares(2)
+        nc.sync.dma_start(y_rows[:, 0:3:2, :], y[:, 0:3:2, :])
         shares(1)
+        nc.sync.dma_start(y_rows[:, 1, :], y[:, 1, :])
         shares(3)
+        nc.sync.dma_start(y_rows[:, 3, :], y[:, 3, :])
 
         y_bf = keep.tile([P, N, PACK], BF16, name="y_bf", align_bytes=64)
         y_codes = keep.tile([P, N], U32, name="y_codes", align_bytes=64)
         y_scales = keep.tile([P, N], U8, name="y_scales", align_bytes=64)
-        y_turned = y[:].rearrange("p i n -> p n i")
-        nc.vector.tensor_copy(y_bf[:, 0:ROUND_SPLIT, :], y_turned[:, 0:ROUND_SPLIT, :])
-        nc.scalar.copy(y_bf[:, ROUND_SPLIT:N, :], y_turned[:, ROUND_SPLIT:N, :])
+        y_from = y[:].rearrange("p i (c e) -> p c i e", e=PACK)
+        y_to = y_bf[:].rearrange("p (c e) i -> p c i e", e=PACK)
+        nc.vector.tensor_copy(y_to[:, 0 : ROUND_SPLIT // PACK], y_from[:, 0 : ROUND_SPLIT // PACK])
+        nc.scalar.copy(y_to[:, ROUND_SPLIT // PACK : N // PACK], y_from[:, ROUND_SPLIT // PACK : N // PACK])
         nc.vector.quantize_mx(y_codes[:].bitcast(E4M3X4), y_scales[:], y_bf[:].rearrange("p n i -> p (n i)"))
         nc.sync.dma_start(out_1[0].rearrange("p c r -> p (c r)").bitcast(I32), y_codes[:].bitcast(I32))
         for q in range(4):

from contextlib import ExitStack

import concourse.mybir as mybir
from concourse.masks import make_identity

K, J, N, T, V = 512, 512, 256, 1024, 1024
FLOPS = 2 * K * J * N

F32 = mybir.dt.float32
BF16 = mybir.dt.bfloat16
U32 = mybir.dt.uint32
I32 = mybir.dt.int32
U16 = mybir.dt.uint16
U8 = mybir.dt.uint8
E5M2X4 = mybir.dt.float8_e5m2_x4
E4M3X4 = mybir.dt.float8_e4m3fn_x4
ALU = mybir.AluOpType
ACT = mybir.ActivationFunctionType
AXIS_X = mybir.AxisListType.X

P = 128
PACK = 4
PAD = 8
LIST_COLS = J // 16
SPLIT_G = (0, 1)
SPLIT_X = (0,)
SUM_ON_TENSOR = (3,)
WEIGH_ON_SCALAR = (1,)
RING = 2
SHARES_ON_SCALAR = (0,)
HALVED = ()
ON_VECTOR = ()
STEPPED_TURN = ()
ROUND_SPLIT = 176


def tile_list_moment_steps_sized_shares_pl_kernel(tc, xf, ra, gt, cb, bn, offs, offs2, out_0, out_1, out_2):
    nc = tc.nc
    with ExitStack() as ctx:
        keep = ctx.enter_context(tc.tile_pool(name="keep", bufs=1))
        turn = ctx.enter_context(tc.psum_pool(name="turn", bufs=5))
        acc = ctx.enter_context(tc.psum_pool(name="acc", bufs=3))

        g_list = keep.tile([P, LIST_COLS], U16, name="g_list")
        x_list = keep.tile([P, LIST_COLS], U16, name="x_list")
        g_tab = [keep.tile([P, V], F32, name=f"g_tab{h}") for h in range(2)]
        x_tab = [keep.tile([P, T], F32, name=f"x_tab{i}") for i in range(PACK)]
        bn_pairs = keep.tile([P, 2], F32, name="bn_pairs")
        cb_sb = keep.tile([P, PACK], F32, name="cb_sb")
        ra_sb = keep.tile([P, PACK], F32, name="ra_sb")

        x_rows = xf.rearrange("(p i) c -> p i c", i=PACK)
        nc.sync.dma_start(g_list[:], offs2)
        for h in range(2):
            nc.sync.dma_start(g_tab[h][:], gt[h * P : (h + 1) * P, :])
        nc.sync.dma_start(x_list[:], offs)
        nc.scalar.dma_start(bn_pairs[:], bn.rearrange("o (p e) -> (o p) e", e=2))
        nc.sync.dma_start(x_tab[0][:], x_rows[:, 0, :])
        nc.sync.dma_start(cb_sb[:], cb.rearrange("(p t) o -> p (t o)", t=PACK))
        nc.sync.dma_start(ra_sb[:], ra.rearrange("o (p t) -> (o p) t", t=PACK))
        for i in range(1, PACK):
            nc.sync.dma_start(x_tab[i][:], x_rows[:, i, :])

        ident = keep.tile([P, P], F32, name="ident")
        make_identity(nc, ident[:])

        bn_ps = turn.tile([P, 2, P], F32, name="bn_ps", tag="turn")
        for e in range(2):
            nc.tensor.transpose(bn_ps[:, e, :], bn_pairs[:, e : e + 1].to_broadcast([P, P]), ident[:])
        bn_row = keep.tile([P, N], F32, name="bn_row")
        nc.vector.tensor_copy(
            out=bn_row[:].rearrange("p (m e) -> p m e", e=2), in_=bn_ps[:].rearrange("p e m -> p m e")
        )

        def gather(dst, table, lst, split):
            half = LIST_COLS // 2
            if split:
                nc.scalar.activation(dst[:, 0 : J // 2], table[:].indirect(lst[:, 0:half]), ACT.Copy)
                nc.vector.tensor_copy(dst[:, J // 2 : J], table[:].indirect(lst[:, half:LIST_COLS]))
            else:
                nc.scalar.activation(dst, table[:].indirect(lst[:]), ACT.Copy)

        g_ps = []
        g_abs0 = keep.tile([P, PACK, P], F32, name="g_abs0")
        g_abs1 = keep.tile([P, PACK, P + PACK], F32, name="g_abs1", tag="shared")
        g_max = keep.tile([P, PACK], F32, name="g_max")
        g_codes = keep.tile([P, N], U32, name="g_codes", align_bytes=64)
        g_scales = keep.tile([P, N], U8, name="g_scales", align_bytes=64)
        y = keep.tile([P, PACK, N], F32, name="y")
        y_rows = out_0.rearrange("(p i) n -> p i n", i=PACK)
        g_picked, x_picked, x_ps, u_codes, u_scales, ew, total = {}, {}, {}, {}, {}, {}, {}

        ring = [keep.tile([P, PAD + J], F32, name=f"picked{b}") for b in range(RING)]
        zero = keep.tile([P, 1], F32, name="zero")
        nc.vector.memset(zero[:], 0.0)
        for b in range(RING):
            nc.scalar.activation(ring[b][:, PAD - 1 : PAD], zero[:], ACT.Copy)

        def pick_g(h):
            g_picked[h] = ring[h % RING]
            gather(g_picked[h][:, PAD : PAD + J], g_tab[h], g_list, h in SPLIT_G)

        def turn_g(h):
            bank = turn.tile([P, PACK, P], F32, name=f"g_ps{h}", tag="turn")
            for t in range(PACK):
                nc.tensor.transpose(bank[:, t, :], g_picked[h][:, PAD + t : PAD + J : PACK], ident[:])
            g_ps.append(bank)
            if h == 0:
                nc.scalar.activation(g_abs0[:], bank[:], ACT.Abs)
                nc.vector.tensor_reduce(g_abs1[:, :, P], g_abs0[:], AXIS_X, ALU.max)
            else:
                nc.scalar.activation(g_abs1[:, :, 0:P], bank[:], ACT.Abs)
                nc.vector.tensor_reduce(g_max[:], g_abs1[:, :, 0 : P + 1], AXIS_X, ALU.max)

        g_fac = keep.tile([P, PACK], F32, name="g_fac")

        def factor_g():
            g_den = keep.tile([P, PACK], F32, name="g_den")
            g_inv = keep.tile([P, PACK], F32, name="g_inv")
            nc.vector.reciprocal(g_inv[:], cb_sb[:])
            nc.vector.scalar_tensor_tensor(g_den[:], g_max[:], 0.2, g_inv[:], ALU.add, ALU.mult)
            nc.vector.reciprocal(g_fac[:], g_den[:])

        def quantise_g():
            g_bf = keep.tile([P, N, PACK], BF16, name="g_bf", align_bytes=64)
            for h in range(2):
                nc.vector.tensor_tensor(
                    g_bf[:, h * P : (h + 1) * P, :],
                    g_ps[h][:].rearrange("p t n -> p n t"),
                    g_fac[:].unsqueeze(1).to_broadcast([P, P, PACK]),
                    ALU.mult,
                )
            nc.vector.quantize_mx(g_codes[:].bitcast(E5M2X4), g_scales[:], g_bf[:].rearrange("p n t -> p (n t)"))

        def pick_x(i):
            x_picked[i] = ring[(2 + i) % RING]
            if i in HALVED:
                for a in range(2):
                    nc.scalar.activation(
                        x_picked[i][:, PAD + a * J // 2 : PAD + (a + 1) * J // 2],
                        x_tab[i][:].indirect(x_list[:, a * LIST_COLS // 2 : (a + 1) * LIST_COLS // 2]),
                        ACT.Copy,
                    )
            elif i in ON_VECTOR:
                nc.vector.tensor_copy(x_picked[i][:, PAD : PAD + J], x_tab[i][:].indirect(x_list[:]))
            else:
                gather(x_picked[i][:, PAD : PAD + J], x_tab[i], x_list, i in SPLIT_X)

        def step_x(i):
            picked = x_picked[i]
            step = keep.tile([P, PACK, P], F32, name=f"step{i}", tag="shared" if i == 1 else f"step{i}")
            before = picked[:, PAD - 1 : PAD - 1 + J].rearrange("p (q t) -> p q t", t=PACK)
            x_ps[i] = turn.tile([P, PACK, P], F32, name=f"x_ps{i}", tag="turn")
            if i in SUM_ON_TENSOR:
                nc.scalar.activation(step[:].rearrange("p t q -> p q t"), before, ACT.Copy, scale=-0.6)
                for t in range(PACK):
                    nc.tensor.matmul(
                        x_ps[i][:, t, :], picked[:, PAD + t : PAD + J : PACK], ident[:],
                        start=(t == 0), stop=False, is_transpose=True,
                    )
                for t in range(PACK):
                    nc.tensor.matmul(
                        x_ps[i][:, t, :], step[:, t, :], ident[:],
                        start=False, stop=(t == PACK - 1), is_transpose=True,
                    )
            elif i in STEPPED_TURN:
                flat = step[:].rearrange("p t q -> p (t q)")
                nc.vector.scalar_tensor_tensor(
                    flat, picked[:, PAD - 1 : PAD - 1 + J], -0.6, picked[:, PAD : PAD + J], ALU.mult, ALU.add
                )
                for t in range(PACK):
                    nc.tensor.transpose(x_ps[i][:, t, :], flat[:, t::PACK], ident[:])
            else:
                parts = 2 if i in HALVED else 1
                for a in range(parts):
                    qs = slice(a * P // parts, (a + 1) * P // parts)
                    nc.vector.scalar_tensor_tensor(
                        step[:].rearrange("p t q -> p q t")[:, qs, :],
                        before[:, qs, :],
                        -0.6,
                        picked[:, PAD : PAD + J].rearrange("p (q t) -> p q t", t=PACK)[:, qs, :],
                        ALU.mult,
                        ALU.add,
                    )
                for t in range(PACK):
                    nc.tensor.transpose(x_ps[i][:, t, :], step[:, t, :], ident[:])

        def quantise_x(i):
            u_bf = keep.tile([P, P, PACK], BF16, name=f"u_bf{i}", align_bytes=64)
            if i in WEIGH_ON_SCALAR:
                planes = keep.tile([P, PACK, P], BF16, name=f"u_planes{i}")
                for t in range(PACK):
                    nc.scalar.activation(planes[:, t, :], x_ps[i][:, t, :], ACT.Copy, scale=ra_sb[:, t : t + 1])
                nc.scalar.copy(
                    u_bf[:].rearrange("p (c e) t -> p c t e", e=PACK), planes[:].rearrange("p t (c e) -> p c t e", e=PACK)
                )
            else:
                nc.vector.tensor_tensor(
                    u_bf[:],
                    x_ps[i][:].rearrange("p t m -> p m t"),
                    ra_sb[:].unsqueeze(1).to_broadcast([P, P, PACK]),
                    ALU.mult,
                )
            u_codes[i] = keep.tile([P, P], U32, name=f"u_codes{i}", align_bytes=64)
            u_scales[i] = keep.tile([P, P], U8, name=f"u_scales{i}", align_bytes=64)
            nc.vector.quantize_mx(
                u_codes[i][:].bitcast(E5M2X4), u_scales[i][:], u_bf[:].rearrange("p m t -> p (m t)")
            )

        def product(i):
            w = acc.tile([P, N], F32, name=f"w{i}", tag="w")
            nc.tensor.matmul_mx(
                out=w[:],
                lhsT=u_codes[i][:].bitcast(E5M2X4),
                lhsT_scale=u_scales[i][:],
                rhs=g_codes[:].bitcast(E5M2X4),
                rhs_scale=g_scales[:],
                start=True,
                stop=True,
            )
            neg_z = keep.tile([P, N], F32, name=f"neg_z{i}")
            nc.vector.scalar_tensor_tensor(neg_z[:], w[:], -0.02, bn_row[:], ALU.mult, ALU.subtract)
            neg_top = keep.tile([P, 1], F32, name=f"neg_top{i}")
            nc.vector.tensor_reduce(neg_top[:], neg_z[:], AXIS_X, ALU.min)
            ew[i] = keep.tile([P, N], F32, name=f"ew{i}")
            total[i] = keep.tile([P, 1], F32, name=f"total{i}")
            nc.scalar.activation(ew[i][:], neg_z[:], ACT.Exp, bias=neg_top[:], scale=-1.0, accum_out=total[i][:])

        def shares(i):
            inv = keep.tile([P, 1], F32, name=f"inv{i}")
            if i in SHARES_ON_SCALAR:
                part = keep.tile([P, 1], F32, name=f"part{i}")
                nc.scalar.activation(part[:], total[i][:], ACT.Copy, scale=1.0 / 256.0)
                nc.vector.reciprocal(inv[:], part[:])
                nc.scalar.activation(y[:, i, :], ew[i][:], ACT.Copy, scale=inv[:])
            else:
                nc.vector.reciprocal(inv[:], total[i][:])
                nc.vector.tensor_scalar(y[:, i, :], ew[i][:], inv[:], 256.0, ALU.mult, ALU.mult)

        pick_g(0)
        turn_g(0)
        pick_g(1)
        turn_g(1)
        factor_g()
        pick_x(0)
        step_x(0)
        quantise_x(0)
        pick_x(1)
        step_x(1)
        pick_x(2)
        step_x(2)
        pick_x(3)
        step_x(3)
        quantise_g()
        quantise_x(2)
        quantise_x(3)
        quantise_x(1)
        product(0)
        product(2)
        product(1)
        product(3)
        shares(0)
        shares(2)
        nc.sync.dma_start(y_rows[:, 0:3:2, :], y[:, 0:3:2, :])
        shares(1)
        nc.sync.dma_start(y_rows[:, 1, :], y[:, 1, :])
        shares(3)
        nc.sync.dma_start(y_rows[:, 3, :], y[:, 3, :])

        y_bf = keep.tile([P, N, PACK], BF16, name="y_bf", align_bytes=64)
        y_codes = keep.tile([P, N], U32, name="y_codes", align_bytes=64)
        y_scales = keep.tile([P, N], U8, name="y_scales", align_bytes=64)
        y_from = y[:].rearrange("p i (c e) -> p c i e", e=PACK)
        y_to = y_bf[:].rearrange("p (c e) i -> p c i e", e=PACK)
        nc.vector.tensor_copy(y_to[:, 0 : ROUND_SPLIT // PACK], y_from[:, 0 : ROUND_SPLIT // PACK])
        nc.scalar.copy(y_to[:, ROUND_SPLIT // PACK : N // PACK], y_from[:, ROUND_SPLIT // PACK : N // PACK])
        nc.vector.quantize_mx(y_codes[:].bitcast(E4M3X4), y_scales[:], y_bf[:].rearrange("p n i -> p (n i)"))
        nc.sync.dma_start(out_1[0].rearrange("p c r -> p (c r)").bitcast(I32), y_codes[:].bitcast(I32))
        for q in range(4):
            queue = nc.scalar if q % 2 == 0 else nc.sync
            queue.dma_start(
                out_2[0, 4 * q : 4 * q + 4, :].bitcast(I32), y_scales[32 * q : 32 * q + 4, :].bitcast(I32)
            )
